import numpy as np, ml_dtypes
CORES = [2,3,42,43,82,83,122,123]
N = 8
import mx_ref
BF = ml_dtypes.bfloat16
def f(rng, *shape):
    return mx_ref.flush((rng.standard_normal(shape, dtype=np.float32) * np.exp2(rng.integers(-2, 3, shape[:-1] + (1,)))).astype(BF))
def wide(rng, *shape, cols=0):
    v = rng.standard_normal(shape, dtype=np.float32) * np.exp2(rng.integers(-12, 13, shape)).astype(np.float32)
    if cols: v *= np.repeat(np.exp2(rng.integers(-cols, cols + 1, shape[:-2] + (1, shape[-1] // 4))) * (rng.random(shape[:-2] + (1, shape[-1] // 4)) > 0.0625), 4, axis=-1).astype(np.float32)
    return mx_ref.flush(v.astype(BF))
PG, PW = 16, 64
def bare(d):
    d["sm"][:, :, 4 * PG:] = 0; d["gs"][:, :, 8:] = 0
    return d
def sizes(rng, d):
    for n in ("sm", "gs"): d[n] = mx_ref.flush((d[n].astype(np.float32) * np.exp2(rng.integers(-12, 13, (N, 1, 1))).astype(np.float32)).astype(BF))
    return d
def setup_inputs(rng):
    return bare({"pg": f(rng, N, 128 * PG, 4 * PW), "sm": f(rng, N, 128, 512), "gs": f(rng, N, 128, 512), "qw": f(rng, N, 128, 1024)})
def setup_inputs_ties(rng):
    d = setup_inputs(rng); v = d["sm"].reshape(N, 128, 128, 4).copy()
    for q in range(N):
        k = rng.integers(PG // 4 + 1, PG // 2 + 1); p = rng.permutation(PG)
        v[q][:, p[k:]] = v[q][:, p[np.arange(k, PG) % k]]
    d["sm"] = v.reshape(N, 128, 512)
    d = sizes(rng, d)
    for r in rng.permutation(N)[:2]: d["gs"][r][:, 4:8] = 0
    return d
def setup_inputs_last(rng):
    d = setup_inputs(rng); c = f(rng, 128, 4)
    for r in range(N):
        j = rng.integers(0, 2)
        d["gs"][r][:, 4 * j:4 * j + 4] = c
        d["sm"][r][:, 4 * PG - 4:4 * PG] = (c.astype(np.float32) * 2).astype(BF)
    return d
def setup_inputs_alike(rng):
    d = setup_inputs(rng); d["gs"] = np.stack([d["gs"][0]] * N); return d
def setup_inputs_below(rng):
    d = setup_inputs(rng)
    d["gs"] = np.abs(d["gs"].astype(np.float32)).astype(BF)
    d["sm"] = (-np.abs(d["sm"].astype(np.float32))).astype(BF)
    return bare(sizes(rng, d))
def setup_inputs_spread(rng):
    d = setup_inputs(rng); d["pg"] = wide(rng, N, 128 * PG, 4 * PW); d["sm"] = wide(rng, N, 128, 512); d["gs"] = wide(rng, N, 128, 512)
    return bare(d)
def check_inputs(d):
    b = []
    for r in range(N):
        if d["sm"][r][:, 4 * PG:].astype(np.float32).any(): b.append("sm")
        if d["gs"][r][:, 8:].astype(np.float32).any(): b.append("gs")
    return b
def reference(pg, sm, gs, qw):
    S = [mx_ref.quantize(t) for t in sm]; G = [mx_ref.quantize(t) for t in gs]
    y = np.zeros((N, 128, 2 * N * PW), np.float32); ch = np.zeros((N, 2, N), np.float32)
    for r in range(N):
        W = [mx_ref.quantize(qw[r][:, 512 * j:512 * j + 512]) for j in range(2)]
        for q in range(N):
            score = mx_ref.matmul(S[q], G[r])
            for j in range(2):
                c = int(np.argmax(score[:PG, j]))
                k = PW * (j * N + q)
                y[r][:, k:k + PW] = mx_ref.matmul(W[j], mx_ref.quantize(pg[q][128 * c:128 * c + 128]))
                ch[r, j, q] = c
    return {"y": y, "ch": ch}

@@ -1,0 +1,316 @@
+from concourse.bass import DstId, RemoteDMATransfer
+from concourse.mybir import dt, AluOpType, AxisListType, ActivationFunctionType
+
+F8 = "float8_e4m3fn_x4"
+SCRATCH = {
+    "gt": ("sbuf", [128, 1024], "bfloat16"),
+    "st": ("sbuf", [128, 512], "bfloat16"),
+    "wt": ("sbuf", [128, 1024], "bfloat16"),
+    "win": ("sbuf", [128, 4096], "bfloat16"),
+    "pt": ("sbuf", [128, 4096], "bfloat16"),
+    "sgc": ("sbuf", [128, 272], F8),
+    "sgs": ("sbuf", [128, 272], "uint8"),
+    "smc": ("sbuf", [128, 128], F8),
+    "sms": ("sbuf", [128, 128], "uint8"),
+    "qwc": ("sbuf", [128, 256], F8),
+    "qws": ("sbuf", [128, 256], "uint8"),
+    "qpc": ("sbuf", [128, 1024], F8),
+    "qps": ("sbuf", [128, 1024], "uint8"),
+    "lc": ("sbuf", [128, 1024], F8),
+    "ls": ("sbuf", [128, 1024], "uint8"),
+    "hc": ("sbuf", [128, 256], F8),
+    "hs": ("sbuf", [128, 256], "uint8"),
+    "ia": ("sbuf", [128, 16], "int32"),
+    "ib": ("sbuf", [128, 16], "int32"),
+    "ic": ("sbuf", [128, 16], "int32"),
+    "bs": ("sbuf", [128, 16], "float32"),
+    "base": ("sbuf", [128, 16], "float32"),
+    "neg": ("sbuf", [128, 16], "float32"),
+    "z32": ("sbuf", [128, 32], "float32"),
+    "run": ("sbuf", [128, 16], "float32"),
+    "lt": ("sbuf", [128, 16], "float32"),
+    "cc": ("sbuf", [128, 1], "float32"),
+    "rep": ("sbuf", [128, 32], "float32"),
+    "cb": ("sbuf", [128, 128], "float32"),
+    "off": ("sbuf", [128, 256], "uint16"),
+    "xch": ("sbuf", [128, 2], "float32"),
+    "ysb": ("sbuf", [128, 1024], "float32"),
+    "chd": ("dram", [8, 128, 1], "float32"),
+}
+for _b in range(8):
+    SCRATCH["ps%d" % _b] = ("psum", [128, 512], "float32")
+
+SEMAPHORES = ["ms", "qz", "lz", "lgs", "qg", "lsm", "qs", "i1", "i2", "b1", "b2", "b3", "lpg", "lqw", "qw", "gsa", "sc",
+              "v1", "v2", "v3", "v4", "v5", "cho", "cha", "l1", "stc", "sty", "stz", "loc", "hcs", "hss", "qown"]
+for _k in range(4):
+    SEMAPHORES += ["oa%d" % _k, "ob%d" % _k, "gv%d" % _k, "gx%d" % _k, "qb%d" % _k,
+                   "my%da" % _k, "my%db" % _k, "ya%d" % _k, "yb%d" % _k]
+for _q in range(8):
+    SEMAPHORES += ["pq%d" % _q]
+
+NP = 4
+CUT = 24
+
+
+def mask_of(eng):
+    m = 0
+    for e in eng:
+        m |= 1 << e
+    return m
+
+
+def did(topo, c):
+    a = topo.addr(c)
+    return DstId(rid=a[0], pnc=a[1])
+
+
+def rounds_of(T, topo):
+    ch = [topo.chip(T.cores[2 * k]) for k in range(NP)]
+    return sorted([1, 2, 3], key=lambda s: (topo.same_plane(ch[0], ch[s]), s))
+
+
+def helpers_of(T, topo, k):
+    a = T.cores[2 * k]
+    far = [c for c in T.cores if topo.chip(c) != topo.chip(a)]
+    return [c for c in topo.cores_of(a) if topo.die(c) != topo.die(a) and all(topo.may_write(c, f) for f in far)]
+
+
+def inner_engines(T, topo, src, dst):
+    far = [c for c in T.cores if topo.chip(c) != topo.chip(src)]
+    out = topo.engines(src, far[0])
+    return [e for e in topo.engines(src, dst) if e not in out]
+
+
+def codes(ap):
+    return ap.bitcast(dt.uint8)
+
+
+def send_pair(g, T, topo, core, q, kd, cbuf, sbuf, base, before_scales=None):
+    dst = [2 * kd, 2 * kd + 1]
+    eng = topo.engines(core, T.cores[dst[0]])
+    half = len(eng) // 2
+    n = 0
+    for what in range(2):
+        if what and before_scales:
+            before_scales()
+        tr = []
+        for h, r in enumerate(dst):
+            a = base + 128 * h
+            if what == 0:
+                s, d = codes(cbuf[:, a:a + 128]), codes(T.lc[:, 128 * q:128 * q + 128])
+            else:
+                s, d = sbuf[:, a:a + 128], T.ls[:, 128 * q:128 * q + 128]
+            tr.append(RemoteDMATransfer(dst_ids=[did(topo, T.cores[r])], dma_engine_mask=mask_of(eng[h * half:(h + 1) * half]),
+                                        remote_sem=T.sem["pq%d" % q], srcs=[s], dsts=[d]))
+        g.remote_dma_fused(tr, local_sem=T.sem.loc)
+        n += 2 * half
+    return n
+
+
+def helper_program(g, core, T, topo, q, kd):
+    n8 = len(inner_engines(T, topo, T.cores[q], core))
+    g.wait_ge(T.sem.hcs, n8)
+    n = send_pair(g, T, topo, core, q, kd, T.hc, T.hs, 0, lambda: g.wait_ge(T.sem.hss, n8))
+    g.wait_ge(T.sem.loc, n)
+
+
+def rank_program(g, core, T, topo):
+    sem = T.sem
+    rounds = rounds_of(T, topo)
+    rank = T.rank_of(core)
+    if rank is None:
+        for k in range(NP):
+            hs = helpers_of(T, topo, k)
+            for h in range(2):
+                if core == hs[h]:
+                    helper_program(g, core, T, topo, 2 * k + h, k ^ rounds[0])
+        return
+    q = rank
+    k0 = q // 2
+    others = [r for r in range(8) if r != q]
+    partner = q ^ 1
+    slot = lambda r, o: 8 if r == o else (r if r < o else r - 1)
+    order = [k0 ^ s for s in rounds] + [k0]
+    V, S, Y, E = g.vector, g.scalar, g.sync, g.tensor
+
+    Y.dma_start(T.gt[:, 0:8], T.gs[:, 0:8]).then_inc(sem.lgs, 16)
+    S.dma_start(T.st[:, 0:64], T.sm[:, 0:64]).then_inc(sem.lsm, 16)
+    for m in range(16):
+        if m == 12:
+            S.wait_ge(sem.qz, 1)
+            S.dma_start(codes(T.sgc[:, 142:144]), codes(T.sgc[:, 0:2])).then_inc(sem.lz, 16)
+            S.dma_start(T.sgs[:, 142:144], T.sgs[:, 0:2]).then_inc(sem.lz, 16)
+        (Y if m < 8 else S).dma_start(T.win[:, 256 * m:256 * m + 256], T.pg[128 * m:128 * m + 128, :]).then_inc(sem.lpg, 16)
+    Y.dma_start(T.wt[:], T.qw[:]).then_inc(sem.lqw, 16)
+
+    g.iota(T.ia[:], [[0, 16]], 0, 1).then_inc(sem.i1, 1)
+    g.iota(T.ib[:], [[16, 16]], 0, 0).then_inc(sem.i2, 1)
+    V.memset(T.gt[:, 8:1024], 0.0).then_inc(sem.ms, 1)
+    V.memset(T.st[:, 64:512], 0.0).then_inc(sem.ms, 1)
+    V.memset(T.neg[:], -9.0e29).then_inc(sem.ms, 1)
+    V.memset(T.z32[:], 0.0).then_inc(sem.ms, 1)
+    V.memset(T.cb[:, 32:128], 0.0).then_inc(sem.ms, 1)
+    V.wait_ge(sem.ms, 5)
+    V.quantize_mx(T.sgc[:, 0:128], T.sgs[:, 0:128], T.gt[:, 512:1024]).then_inc(sem.qz, 1)
+    V.wait_ge(sem.i1, 1)
+    V.tensor_scalar(T.ic[:], T.ia[:], 15, None, AluOpType.bitwise_and).then_inc(sem.b1, 1)
+    V.wait_ge(sem.i2, 1)
+    V.wait_ge(sem.b1, 1)
+    V.tensor_tensor(T.bs[:], T.ic[:], T.ib[:], AluOpType.add).then_inc(sem.b2, 1)
+    V.wait_ge(sem.b2, 1)
+    V.tensor_scalar(T.base[:], T.bs[:], 1.0 / 256.0, None, AluOpType.mult).then_inc(sem.b3, 1)
+    V.wait_ge(sem.lgs, 16)
+    V.quantize_mx(T.sgc[:, 144:272], T.sgs[:, 144:272], T.gt[:, 0:512]).then_inc(sem.qg, 1)
+    V.wait_ge(sem.lsm, 16)
+    V.quantize_mx(T.smc[:], T.sms[:], T.st[:]).then_inc(sem.qs, 1)
+
+    nloc = 0
+    eng = [e for e in topo.engines(core, T.cores[partner]) if all(e in topo.engines(core, T.cores[r]) for r in others)]
+    ids = [did(topo, T.cores[r]) for r in others]
+    at = [128 + 2 * slot(q, r) for r in others]
+    g.wait_ge(sem.qg, 1)
+    g.remote_dma_fused([RemoteDMATransfer(dst_ids=ids, dma_engine_mask=mask_of(eng), remote_sem=sem.gsa,
+                                          srcs=[codes(T.sgc[:, 144:146])], dsts=[codes(T.sgc[:, a:a + 2]) for a in at])],
+                       local_sem=sem.loc)
+    g.remote_dma_fused([RemoteDMATransfer(dst_ids=ids, dma_engine_mask=mask_of(eng), remote_sem=sem.gsa,
+                                          srcs=[T.sgs[:, 144:146]], dsts=[T.sgs[:, a:a + 2] for a in at])],
+                       local_sem=sem.loc)
+    nloc += 2 * len(eng)
+
+    E.wait_ge(sem.qz, 1)
+    E.wait_ge(sem.lz, 32)
+    E.wait_ge(sem.qg, 1)
+    E.wait_ge(sem.qs, 1)
+    E.wait_ge(sem.gsa, 7 * 2 * len(eng))
+    score = T["ps%d" % (2 * k0)]
+    for b in range(4):
+        a = 128 - 32 * b
+        i = E.matmul_mx(score[:, 0:128], T.sgc[:, a:a + 128], T.sgs[:, a:a + 128], T.smc[:, 0:128], T.sms[:, 0:128], b == 0, b == 3)
+    i.then_inc(sem.sc, 1)
+
+    V.wait_ge(sem.sc, 1)
+    V.tensor_tensor_scan(T.run[:], score[:, 0:16], T.neg[:], -9.0e29, AluOpType.max, AluOpType.max).then_inc(sem.v1, 1)
+    V.wait_ge(sem.v1, 1)
+    V.tensor_scalar(T.lt[:], T.run[:], T.run[:, 15:16], None, AluOpType.is_lt).then_inc(sem.v2, 1)
+    V.wait_ge(sem.v2, 1)
+    V.tensor_reduce(T.cc[:, 0:1], T.lt[:], AxisListType.X, AluOpType.add).then_inc(sem.v3, 1)
+    V.wait_ge(sem.v3, 1)
+    V.tensor_scalar(T.rep[:], T.z32[:], T.cc[:, 0:1], None, AluOpType.add).then_inc(sem.v4, 1)
+    V.wait_ge(sem.v4, 1)
+    V.transpose(T.cb[:, 0:32], T.rep[:]).then_inc(sem.v5, 1)
+    V.wait_ge(sem.v5, 1)
+    V.wait_ge(sem.b3, 1)
+
+    def lists(n):
+        k = order[n]
+        for x in (3, 2, 1, 0):
+            r, j = 2 * k + x // 2, x % 2
+            i = 2 * slot(r, q) + j
+            o = 16 * (4 * k + x)
+            V.tensor_scalar(T.off[:, o:o + 16], T.base[:], T.cb[:, i:i + 1], 256.0, AluOpType.add, AluOpType.mult).then_inc(
+                sem["oa%d" % n] if x else sem["ob%d" % n], 1)
+
+    lists(0)
+    for n in range(4):
+        k = order[n]
+        o = 64 * k
+        if n == 0:
+            V.wait_ge(sem.lpg, 256)
+            S.wait_ge(sem.lpg, 256)
+        V.wait_ge(sem["oa%d" % n], 3)
+        V.wait_ge(sem["ob%d" % n], 1)
+        V.tensor_copy(T.pt[:, 16 * o:16 * (o + CUT)], T.win[:, 0:4096].indirect(T.off[:, o:o + CUT])).then_inc(sem["gv%d" % n], 1)
+        S.wait_ge(sem["oa%d" % n], 3)
+        S.activation(T.pt[:, 16 * (o + CUT):16 * (o + 64)], T.win[:, 0:4096].indirect(T.off[:, o + CUT:o + 64]),
+                     ActivationFunctionType.Copy).then_inc(sem["gx%d" % n], 1)
+        if n < 3:
+            lists(n + 1)
+        V.wait_ge(sem["gv%d" % n], 1)
+        V.wait_ge(sem["gx%d" % n], 1)
+        if n < 3:
+            V.quantize_mx(T.qpc[:, 256 * k:256 * k + 256], T.qps[:, 256 * k:256 * k + 256],
+                          T.pt[:, 1024 * k:1024 * k + 1024]).then_inc(sem["qb%d" % n], 1)
+        else:
+            r = partner
+            V.quantize_mx(T.qpc[:, 128 * r:128 * r + 128], T.qps[:, 128 * r:128 * r + 128],
+                          T.pt[:, 512 * r:512 * r + 512]).then_inc(sem["qb%d" % n], 1)
+            V.quantize_mx(T.lc[:, 128 * q:128 * q + 128], T.ls[:, 128 * q:128 * q + 128],
+                          T.pt[:, 512 * q:512 * q + 512]).then_inc(sem.qown, 1)
+    V.wait_ge(sem.lqw, 16)
+    V.quantize_mx(T.qwc[:], T.qws[:], T.wt[:]).then_inc(sem.qw, 1)
+
+    Y.wait_ge(sem.v5, 1)
+    Y.wait_ge(sem.ms, 5)
+    Y.dma_start(T.chd[q], T.cb[0:1, 0:128]).then_inc(sem.cho, 16)
+    Y.dma_start(T.xch[q:q + 1, 0:2], T.cb[0:1, 16:18]).then_inc(sem.l1, 16)
+    nl1 = 16
+
+    hk = helpers_of(T, topo, k0)[q % 2]
+    for n in range(4):
+        k = order[n]
+        g.wait_ge(sem["qb%d" % n], 1)
+        if n in (1, 2):
+            nloc += send_pair(g, T, topo, core, q, k, T.qpc, T.qps, 256 * k)
+        else:
+            dst = hk if n == 0 else T.cores[partner]
+            ie = inner_engines(T, topo, core, dst)
+            rid, pid = topo.addr(dst)[0:2]
+            if n == 0:
+                a, w = 256 * k, 256
+                d, ds, s1, s2 = T.hc[:, 0:256], T.hs[:, 0:256], sem.hcs, sem.hss
+            else:
+                a, w = 128 * partner, 128
+                d, ds = T.lc[:, 128 * q:128 * q + 128], T.ls[:, 128 * q:128 * q + 128]
+                s1 = s2 = sem["pq%d" % q]
+            g.remote_dma(codes(d), codes(T.qpc[:, a:a + w]), s1, sem.loc, pid, rid, mask_of(ie))
+            g.remote_dma(ds, T.qps[:, a:a + w], s2, sem.loc, pid, rid, mask_of(ie))
+            nloc += 2 * len(ie)
+        if n == 1:
+            g.wait_ge(sem.cho, 16)
+            g.remote_dma_fused([RemoteDMATransfer(dst_ids=ids, dma_engine_mask=mask_of(eng[:1]), remote_sem=sem.cha,
+                                                  srcs=[T.chd[q]], dsts=[T.chd[q] for r in others])], local_sem=sem.loc)
+            nloc += 1
+
+    arrive = [order[1], order[3], order[2], order[0]]
+    E.wait_ge(sem.qw, 1)
+    for n, k in enumerate(arrive):
+        if k == k0:
+            E.wait_ge(sem.qown, 1)
+            E.wait_ge(sem["pq%d" % partner], 2 * len(inner_engines(T, topo, T.cores[partner], core)))
+        else:
+            for o in (2 * k, 2 * k + 1):
+                E.wait_ge(sem["pq%d" % o], len(topo.engines(T.cores[o], core)))
+        for j in range(2):
+            E.matmul_mx(T["ps%d" % (2 * k + j)][:, 0:256], T.qwc[:, 128 * j:128 * j + 128], T.qws[:, 128 * j:128 * j + 128],
+                        T.lc[:, 256 * k:256 * k + 256], T.ls[:, 256 * k:256 * k + 256], True, True).then_inc(
+                            sem["my%d%s" % (k, "ab"[j])], 1)
+        V.wait_ge(sem["my%da" % k], 1)
+        S.wait_ge(sem["my%db" % k], 1)
+        for h in range(2):
+            o = 2 * k + h
+            V.tensor_copy(T.ysb[:, 64 * o:64 * o + 64], T["ps%d" % (2 * k)][:, 128 * h:128 * h + 64]).then_inc(sem["ya%d" % k], 1)
+            S.activation(T.ysb[:, 64 * (8 + o):64 * (8 + o) + 64], T["ps%d" % (2 * k + 1)][:, 128 * h + 64:128 * h + 128],
+                         ActivationFunctionType.Copy).then_inc(sem["yb%d" % k], 1)
+        if n == 0:
+            Y.wait_ge(sem.cha, 7)
+            if q > 0:
+                a = 2 * (q - 1)
+                Y.dma_start(T.xch[0:q, 0:2], T.chd[0:q, a:a + 2, 0]).then_inc(sem.l1, 16)
+                nl1 += 16
+            if q < 7:
+                a = 2 * q
+                Y.dma_start(T.xch[q + 1:8, 0:2], T.chd[q + 1:8, a:a + 2, 0]).then_inc(sem.l1, 16)
+                nl1 += 16
+        c = 128 * k
+        Y.wait_ge(sem["ya%d" % k], 2)
+        Y.dma_start(T.y[:, c:c + 128], T.ysb[:, c:c + 128]).then_inc(sem.sty, 16)
+        S.wait_ge(sem["yb%d" % k], 2)
+        S.dma_start(T.y[:, 512 + c:512 + c + 128], T.ysb[:, 512 + c:512 + c + 128]).then_inc(sem.stz, 16)
+        if n == 1:
+            Y.wait_ge(sem.l1, nl1)
+            for j in range(2):
+                Y.dma_start(T.ch[j:j + 1, :], T.xch[0:8, j:j + 1]).then_inc(sem.stc, 16)
+    Y.wait_ge(sem.sty, 64)
+    Y.wait_ge(sem.stc, 32)
+    S.wait_ge(sem.stz, 64)
+    g.wait_ge(sem.loc, nloc)

@@ -1,15 +1,18 @@
 from concourse.bass import DstId, RemoteDMATransfer
-from concourse.mybir import dt, AluOpType, AxisListType, ActivationFunctionType
+from concourse.mybir import dt, AluOpType, ActivationFunctionType
 
 F8 = "float8_e4m3fn_x4"
 SCRATCH = {
-    "gt": ("sbuf", [128, 1024], "bfloat16"),
+    "gt": ("sbuf", [128, 512], "bfloat16"),
+    "gz": ("sbuf", [128, 512], "bfloat16"),
     "st": ("sbuf", [128, 512], "bfloat16"),
     "wt": ("sbuf", [128, 1024], "bfloat16"),
     "win": ("sbuf", [128, 4096], "bfloat16"),
     "pt": ("sbuf", [128, 4096], "bfloat16"),
-    "sgc": ("sbuf", [128, 272], F8),
-    "sgs": ("sbuf", [128, 272], "uint8"),
+    "sgc": ("sbuf", [128, 160], F8),
+    "sgs": ("sbuf", [128, 160], "uint8"),
+    "zc": ("sbuf", [128, 128], F8),
+    "zs": ("sbuf", [128, 128], "uint8"),
     "smc": ("sbuf", [128, 128], F8),
     "sms": ("sbuf", [128, 128], "uint8"),
     "qwc": ("sbuf", [128, 256], F8),
@@ -18,8 +21,8 @@ SCRATCH = {
     "qps": ("sbuf", [128, 1024], "uint8"),
     "lc": ("sbuf", [128, 1024], F8),
     "ls": ("sbuf", [128, 1024], "uint8"),
-    "hc": ("sbuf", [128, 256], F8),
-    "hs": ("sbuf", [128, 256], "uint8"),
+    "hc": ("sbuf", [128, 384], F8),
+    "hs": ("sbuf", [128, 384], "uint8"),
     "ia": ("sbuf", [128, 16], "int32"),
     "ib": ("sbuf", [128, 16], "int32"),
     "ic": ("sbuf", [128, 16], "int32"),
@@ -27,6 +30,7 @@ SCRATCH = {
     "base": ("sbuf", [128, 16], "float32"),
     "neg": ("sbuf", [128, 16], "float32"),
     "z32": ("sbuf", [128, 32], "float32"),
+    "sct": ("sbuf", [128, 32], "float32"),
     "run": ("sbuf", [128, 16], "float32"),
     "lt": ("sbuf", [128, 16], "float32"),
     "cc": ("sbuf", [128, 1], "float32"),
@@ -40,16 +44,18 @@ SCRATCH = {
 for _b in range(8):
     SCRATCH["ps%d" % _b] = ("psum", [128, 512], "float32")
 
-SEMAPHORES = ["ms", "qz", "lz", "lgs", "qg", "lsm", "qs", "i1", "i2", "b1", "b2", "b3", "lpg", "lqw", "qw", "gsa", "sc",
-              "v1", "v2", "v3", "v4", "v5", "cho", "cha", "l1", "stc", "sty", "stz", "loc", "hcs", "hss", "qown"]
-for _k in range(4):
-    SEMAPHORES += ["oa%d" % _k, "ob%d" % _k, "gv%d" % _k, "gx%d" % _k, "qb%d" % _k,
-                   "my%da" % _k, "my%db" % _k, "ya%d" % _k, "yb%d" % _k]
-for _q in range(8):
-    SEMAPHORES += ["pq%d" % _q]
+SEMAPHORES = ["mz", "ms", "qz", "lgs", "qg", "lsm", "cps", "qs", "i1", "i2", "b1", "b2", "b3", "lpg", "lqw", "qw", "gsa", "go",
+              "sc", "v0", "v1", "v3", "v4", "v5", "cho", "cha", "l1", "stc", "sty", "stz", "loc"]
+for _i in range(8):
+    SEMAPHORES += ["oa%d" % _i, "gv%d" % _i, "gx%d" % _i, "qb%d" % _i, "my%da" % _i, "my%db" % _i, "ya%d" % _i, "yb%d" % _i,
+                   "pq%d" % _i]
+for _n in range(3):
+    SEMAPHORES += ["hc%d" % _n, "hs%d" % _n]
 
 NP = 4
-CUT = 24
+CUT = 10
+FIRST = 14
+OWN = 9
 
 
 def mask_of(eng):
@@ -69,15 +75,22 @@ def rounds_of(T, topo):
     return sorted([1, 2, 3], key=lambda s: (topo.same_plane(ch[0], ch[s]), s))
 
 
+def far_of(T, topo, c):
+    return [f for f in T.cores if topo.chip(f) != topo.chip(c)]
+
+
 def helpers_of(T, topo, k):
     a = T.cores[2 * k]
-    far = [c for c in T.cores if topo.chip(c) != topo.chip(a)]
-    return [c for c in topo.cores_of(a) if topo.die(c) != topo.die(a) and all(topo.may_write(c, f) for f in far)]
+    return [c for c in topo.cores_of(a) if topo.die(c) != topo.die(a) and all(topo.may_write(c, f) for f in far_of(T, topo, a))]
+
+
+def outer_engines(T, topo, src):
+    far = far_of(T, topo, src)
+    return [e for e in topo.engines(src, far[0]) if all(e in topo.engines(src, f) for f in far)]
 
 
 def inner_engines(T, topo, src, dst):
-    far = [c for c in T.cores if topo.chip(c) != topo.chip(src)]
-    out = topo.engines(src, far[0])
+    out = outer_engines(T, topo, src)
     return [e for e in topo.engines(src, dst) if e not in out]
 
 
@@ -85,33 +98,36 @@ def codes(ap):
     return ap.bitcast(dt.uint8)
 
 
-def send_pair(g, T, topo, core, q, kd, cbuf, sbuf, base, before_scales=None):
-    dst = [2 * kd, 2 * kd + 1]
-    eng = topo.engines(core, T.cores[dst[0]])
-    half = len(eng) // 2
-    n = 0
-    for what in range(2):
-        if what and before_scales:
-            before_scales()
-        tr = []
-        for h, r in enumerate(dst):
-            a = base + 128 * h
-            if what == 0:
-                s, d = codes(cbuf[:, a:a + 128]), codes(T.lc[:, 128 * q:128 * q + 128])
-            else:
-                s, d = sbuf[:, a:a + 128], T.ls[:, 128 * q:128 * q + 128]
-            tr.append(RemoteDMATransfer(dst_ids=[did(topo, T.cores[r])], dma_engine_mask=mask_of(eng[h * half:(h + 1) * half]),
-                                        remote_sem=T.sem["pq%d" % q], srcs=[s], dsts=[d]))
-        g.remote_dma_fused(tr, local_sem=T.sem.loc)
-        n += 2 * half
+def write(g, topo, dst, d, s, rsem, lsem, eng):
+    rid, pid = topo.addr(dst)[0:2]
+    g.remote_dma(d, s, rsem, lsem, pid, rid, mask_of(eng))
+    return len(eng)
+
+
+def zeros_to(g, T, topo, dst, col, eng):
+    sem = T.sem
+    g.vector.memset(T.gz[:], 0.0).then_inc(sem.mz, 1)
+    g.vector.wait_ge(sem.mz, 1)
+    g.vector.quantize_mx(T.zc[:], T.zs[:], T.gz[:]).then_inc(sem.qz, 1)
+    g.wait_ge(sem.qz, 1)
+    n = write(g, topo, dst, codes(T.sgc[:, col:col + 2]), codes(T.zc[:, 0:2]), sem.gsa, sem.loc, eng)
+    n += write(g, topo, dst, T.sgs[:, col:col + 2], T.zs[:, 0:2], sem.gsa, sem.loc, eng)
     return n
 
 
-def helper_program(g, core, T, topo, q, kd):
+def helper_program(g, core, T, topo, q, rounds):
+    sem = T.sem
+    out = outer_engines(T, topo, core)
     n8 = len(inner_engines(T, topo, T.cores[q], core))
-    g.wait_ge(T.sem.hcs, n8)
-    n = send_pair(g, T, topo, core, q, kd, T.hc, T.hs, 0, lambda: g.wait_ge(T.sem.hss, n8))
-    g.wait_ge(T.sem.loc, n)
+    nloc = zeros_to(g, T, topo, T.cores[q], FIRST + 16, out)
+    for n in range(3):
+        r = 2 * ((q // 2) ^ rounds[n]) + 1 - q % 2
+        a, b = 128 * n, 128 * q
+        g.wait_ge(sem["hc%d" % n], n8)
+        nloc += write(g, topo, T.cores[r], codes(T.lc[:, b:b + 128]), codes(T.hc[:, a:a + 128]), sem["pq%d" % q], sem.loc, out)
+        g.wait_ge(sem["hs%d" % n], n8)
+        nloc += write(g, topo, T.cores[r], T.ls[:, b:b + 128], T.hs[:, a:a + 128], sem["pq%d" % q], sem.loc, out)
+    g.wait_ge(sem.loc, nloc)
 
 
 def rank_program(g, core, T, topo):
@@ -123,35 +139,70 @@ def rank_program(g, core, T, topo):
             hs = helpers_of(T, topo, k)
             for h in range(2):
                 if core == hs[h]:
-                    helper_program(g, core, T, topo, 2 * k + h, k ^ rounds[0])
+                    helper_program(g, core, T, topo, 2 * k + h, rounds)
         return
     q = rank
-    k0 = q // 2
-    others = [r for r in range(8) if r != q]
+    k0, par = q // 2, q % 2
     partner = q ^ 1
-    slot = lambda r, o: 8 if r == o else (r if r < o else r - 1)
-    order = [k0 ^ s for s in rounds] + [k0]
+    hk = helpers_of(T, topo, k0)[par]
+    slot = lambda r, o: OWN if r == o else (r if r < o else r - 1)
+    others = [r for r in range(8) if r != q]
+    far = [r for r in others if r != partner]
+    out = outer_engines(T, topo, core)
+    inp = inner_engines(T, topo, core, T.cores[partner])
+    inh = inner_engines(T, topo, core, hk)
     V, S, Y, E = g.vector, g.scalar, g.sync, g.tensor
+    H = [2 * (k0 ^ s) + 1 - par for s in rounds]
+    D = [2 * (k0 ^ s) + par for s in rounds]
+    seq = [H[0], D[0], H[1], D[1], H[2], D[2], partner, q]
+
+    def page(eng, m):
+        eng.dma_start(T.win[:, 256 * m:256 * m + 256], T.pg[128 * m:128 * m + 128, :]).then_inc(sem.lpg, 16)
 
     Y.dma_start(T.gt[:, 0:8], T.gs[:, 0:8]).then_inc(sem.lgs, 16)
     S.dma_start(T.st[:, 0:64], T.sm[:, 0:64]).then_inc(sem.lsm, 16)
-    for m in range(16):
-        if m == 12:
-            S.wait_ge(sem.qz, 1)
-            S.dma_start(codes(T.sgc[:, 142:144]), codes(T.sgc[:, 0:2])).then_inc(sem.lz, 16)
-            S.dma_start(T.sgs[:, 142:144], T.sgs[:, 0:2]).then_inc(sem.lz, 16)
-        (Y if m < 8 else S).dma_start(T.win[:, 256 * m:256 * m + 256], T.pg[128 * m:128 * m + 128, :]).then_inc(sem.lpg, 16)
+    for m in range(4):
+        page(Y, m)
+        page(S, 4 + m)
+    Y.wait_ge(sem.go, 1)
+    S.wait_ge(sem.go, 1)
+    for m in range(8, 12):
+        page(Y, m)
+        page(S, 4 + m)
     Y.dma_start(T.wt[:], T.qw[:]).then_inc(sem.lqw, 16)
 
-    g.iota(T.ia[:], [[0, 16]], 0, 1).then_inc(sem.i1, 1)
-    g.iota(T.ib[:], [[16, 16]], 0, 0).then_inc(sem.i2, 1)
-    V.memset(T.gt[:, 8:1024], 0.0).then_inc(sem.ms, 1)
+    nloc = zeros_to(g, T, topo, T.cores[partner], FIRST + 14, topo.engines(core, T.cores[partner]))
+    V.memset(T.gt[:, 8:512], 0.0).then_inc(sem.ms, 1)
     V.memset(T.st[:, 64:512], 0.0).then_inc(sem.ms, 1)
     V.memset(T.neg[:], -9.0e29).then_inc(sem.ms, 1)
     V.memset(T.z32[:], 0.0).then_inc(sem.ms, 1)
     V.memset(T.cb[:, 32:128], 0.0).then_inc(sem.ms, 1)
     V.wait_ge(sem.ms, 5)
-    V.quantize_mx(T.sgc[:, 0:128], T.sgs[:, 0:128], T.gt[:, 512:1024]).then_inc(sem.qz, 1)
+    V.wait_ge(sem.lgs, 16)
+    V.quantize_mx(T.sgc[:, 32:160], T.sgs[:, 32:160], T.gt[:]).then_inc(sem.qg, 1)
+    V.wait_ge(sem.lsm, 16)
+    for b in range(1, 4):
+        V.tensor_copy(T.st[:, 128 * b:128 * b + 64], T.st[:, 0:64]).then_inc(sem.cps, 1)
+    V.wait_ge(sem.cps, 3)
+    V.quantize_mx(T.smc[:], T.sms[:], T.st[:]).then_inc(sem.qs, 1)
+
+    g.wait_ge(sem.qg, 1)
+    for what in range(2):
+        tr = []
+        for dst, eng in ((far, out), ([partner], inp)):
+            at = [FIRST + 2 * slot(q, r) for r in dst]
+            if what == 0:
+                s, d = codes(T.sgc[:, 32:34]), [codes(T.sgc[:, a:a + 2]) for a in at]
+            else:
+                s, d = T.sgs[:, 32:34], [T.sgs[:, a:a + 2] for a in at]
+            tr.append(RemoteDMATransfer(dst_ids=[did(topo, T.cores[r]) for r in dst], dma_engine_mask=mask_of(eng),
+                                        remote_sem=sem.gsa, srcs=[s], dsts=d))
+            nloc += len(eng)
+        g.remote_dma_fused(tr, local_sem=sem.loc)
+    g.sem_inc(sem.go, 1)
+
+    g.iota(T.ia[:], [[0, 16]], 0, 1).then_inc(sem.i1, 1)
+    g.iota(T.ib[:], [[16, 16]], 0, 0).then_inc(sem.i2, 1)
     V.wait_ge(sem.i1, 1)
     V.tensor_scalar(T.ic[:], T.ia[:], 15, None, AluOpType.bitwise_and).then_inc(sem.b1, 1)
     V.wait_ge(sem.i2, 1)
@@ -159,157 +210,151 @@ def rank_program(g, core, T, topo):
     V.tensor_tensor(T.bs[:], T.ic[:], T.ib[:], AluOpType.add).then_inc(sem.b2, 1)
     V.wait_ge(sem.b2, 1)
     V.tensor_scalar(T.base[:], T.bs[:], 1.0 / 256.0, None, AluOpType.mult).then_inc(sem.b3, 1)
-    V.wait_ge(sem.lgs, 16)
-    V.quantize_mx(T.sgc[:, 144:272], T.sgs[:, 144:272], T.gt[:, 0:512]).then_inc(sem.qg, 1)
-    V.wait_ge(sem.lsm, 16)
-    V.quantize_mx(T.smc[:], T.sms[:], T.st[:]).then_inc(sem.qs, 1)
+    V.wait_ge(sem.b3, 1)
 
-    nloc = 0
-    eng = [e for e in topo.engines(core, T.cores[partner]) if all(e in topo.engines(core, T.cores[r]) for r in others)]
-    ids = [did(topo, T.cores[r]) for r in others]
-    at = [128 + 2 * slot(q, r) for r in others]
-    g.wait_ge(sem.qg, 1)
-    g.remote_dma_fused([RemoteDMATransfer(dst_ids=ids, dma_engine_mask=mask_of(eng), remote_sem=sem.gsa,
-                                          srcs=[codes(T.sgc[:, 144:146])], dsts=[codes(T.sgc[:, a:a + 2]) for a in at])],
-                       local_sem=sem.loc)
-    g.remote_dma_fused([RemoteDMATransfer(dst_ids=ids, dma_engine_mask=mask_of(eng), remote_sem=sem.gsa,
-                                          srcs=[T.sgs[:, 144:146]], dsts=[T.sgs[:, a:a + 2] for a in at])],
-                       local_sem=sem.loc)
-    nloc += 2 * len(eng)
-
-    E.wait_ge(sem.qz, 1)
-    E.wait_ge(sem.lz, 32)
+    narr = 0
+    for r in far:
+        narr += 2 * len(outer_engines(T, topo, T.cores[r]))
+    narr += 2 * len(inner_engines(T, topo, T.cores[partner], core)) + 2 * len(topo.engines(T.cores[partner], core))
+    narr += 2 * len(outer_engines(T, topo, hk))
     E.wait_ge(sem.qg, 1)
     E.wait_ge(sem.qs, 1)
-    E.wait_ge(sem.gsa, 7 * 2 * len(eng))
-    score = T["ps%d" % (2 * k0)]
-    for b in range(4):
-        a = 128 - 32 * b
-        i = E.matmul_mx(score[:, 0:128], T.sgc[:, a:a + 128], T.sgs[:, a:a + 128], T.smc[:, 0:128], T.sms[:, 0:128], b == 0, b == 3)
-    i.then_inc(sem.sc, 1)
+    E.wait_ge(sem.gsa, narr)
+    score = T.ps6
+    E.matmul_mx(score[:, 0:128], T.smc[:], T.sms[:], T.sgc[:, FIRST:FIRST + 128], T.sgs[:, FIRST:FIRST + 128], True, True).then_inc(
+        sem.sc, 1)
 
     V.wait_ge(sem.sc, 1)
-    V.tensor_tensor_scan(T.run[:], score[:, 0:16], T.neg[:], -9.0e29, AluOpType.max, AluOpType.max).then_inc(sem.v1, 1)
-    V.wait_ge(sem.v1, 1)
-    V.tensor_scalar(T.lt[:], T.run[:], T.run[:, 15:16], None, AluOpType.is_lt).then_inc(sem.v2, 1)
-    V.wait_ge(sem.v2, 1)
-    V.tensor_reduce(T.cc[:, 0:1], T.lt[:], AxisListType.X, AluOpType.add).then_inc(sem.v3, 1)
+    V.transpose(T.sct[:], score[:, 0:32]).then_inc(sem.v0, 1)
+    V.wait_ge(sem.v0, 1)
+    V.tensor_tensor_scan(T.run[:], T.sct[:, 0:16], T.neg[:], -9.0e29, AluOpType.max, AluOpType.max).then_inc(sem.v1, 1)
+    S.wait_ge(sem.v1, 1)
+    S.activation(T.lt[:], T.run[:], ActivationFunctionType.Sign, bias=T.run[:, 15:16], scale=-1.0,
+                 accum_out=T.cc[:, 0:1]).then_inc(sem.v3, 1)
     V.wait_ge(sem.v3, 1)
     V.tensor_scalar(T.rep[:], T.z32[:], T.cc[:, 0:1], None, AluOpType.add).then_inc(sem.v4, 1)
     V.wait_ge(sem.v4, 1)
     V.transpose(T.cb[:, 0:32], T.rep[:]).then_inc(sem.v5, 1)
     V.wait_ge(sem.v5, 1)
-    V.wait_ge(sem.b3, 1)
 
-    def lists(n):
-        k = order[n]
-        for x in (3, 2, 1, 0):
-            r, j = 2 * k + x // 2, x % 2
-            i = 2 * slot(r, q) + j
-            o = 16 * (4 * k + x)
-            V.tensor_scalar(T.off[:, o:o + 16], T.base[:], T.cb[:, i:i + 1], 256.0, AluOpType.add, AluOpType.mult).then_inc(
-                sem["oa%d" % n] if x else sem["ob%d" % n], 1)
+    def lists(i):
+        r = seq[i]
+        for j in range(2):
+            c, o = 2 * slot(r, q) + j, 32 * r + 16 * j
+            V.tensor_scalar(T.off[:, o:o + 16], T.base[:], T.cb[:, c:c + 1], 256.0, AluOpType.add,
+                            AluOpType.mult).then_inc(sem["oa%d" % i], 1)
 
     lists(0)
-    for n in range(4):
-        k = order[n]
-        o = 64 * k
-        if n == 0:
+    for i, r in enumerate(seq):
+        o = 32 * r
+        if i == 0:
             V.wait_ge(sem.lpg, 256)
             S.wait_ge(sem.lpg, 256)
-        V.wait_ge(sem["oa%d" % n], 3)
-        V.wait_ge(sem["ob%d" % n], 1)
-        V.tensor_copy(T.pt[:, 16 * o:16 * (o + CUT)], T.win[:, 0:4096].indirect(T.off[:, o:o + CUT])).then_inc(sem["gv%d" % n], 1)
-        S.wait_ge(sem["oa%d" % n], 3)
-        S.activation(T.pt[:, 16 * (o + CUT):16 * (o + 64)], T.win[:, 0:4096].indirect(T.off[:, o + CUT:o + 64]),
-                     ActivationFunctionType.Copy).then_inc(sem["gx%d" % n], 1)
-        if n < 3:
-            lists(n + 1)
-        V.wait_ge(sem["gv%d" % n], 1)
-        V.wait_ge(sem["gx%d" % n], 1)
-        if n < 3:
-            V.quantize_mx(T.qpc[:, 256 * k:256 * k + 256], T.qps[:, 256 * k:256 * k + 256],
-                          T.pt[:, 1024 * k:1024 * k + 1024]).then_inc(sem["qb%d" % n], 1)
-        else:
-            r = partner
-            V.quantize_mx(T.qpc[:, 128 * r:128 * r + 128], T.qps[:, 128 * r:128 * r + 128],
-                          T.pt[:, 512 * r:512 * r + 512]).then_inc(sem["qb%d" % n], 1)
-            V.quantize_mx(T.lc[:, 128 * q:128 * q + 128], T.ls[:, 128 * q:128 * q + 128],
-                          T.pt[:, 512 * q:512 * q + 512]).then_inc(sem.qown, 1)
-    V.wait_ge(sem.lqw, 16)
-    V.quantize_mx(T.qwc[:], T.qws[:], T.wt[:]).then_inc(sem.qw, 1)
+        V.wait_ge(sem["oa%d" % i], 2)
+        V.tensor_copy(T.pt[:, 16 * o:16 * (o + CUT)], T.win[:, 0:4096].indirect(T.off[:, o:o + CUT])).then_inc(sem["gv%d" % i], 1)
+        S.wait_ge(sem["oa%d" % i], 2)
+        S.activation(T.pt[:, 16 * (o + CUT):16 * (o + 32)], T.win[:, 0:4096].indirect(T.off[:, o + CUT:o + 32]),
+                     ActivationFunctionType.Copy).then_inc(sem["gx%d" % i], 1)
+        if i < 7:
+            lists(i + 1)
+        V.wait_ge(sem["gv%d" % i], 1)
+        V.wait_ge(sem["gx%d" % i], 1)
+        c, s = (T.lc, T.ls) if r == q else (T.qpc, T.qps)
+        V.quantize_mx(c[:, 128 * r:128 * r + 128], s[:, 128 * r:128 * r + 128],
+                      T.pt[:, 512 * r:512 * r + 512]).then_inc(sem["qb%d" % i], 1)
+        if i == 5:
+            V.wait_ge(sem.lqw, 16)
+            V.quantize_mx(T.qwc[:], T.qws[:], T.wt[:]).then_inc(sem.qw, 1)
 
     Y.wait_ge(sem.v5, 1)
     Y.wait_ge(sem.ms, 5)
     Y.dma_start(T.chd[q], T.cb[0:1, 0:128]).then_inc(sem.cho, 16)
-    Y.dma_start(T.xch[q:q + 1, 0:2], T.cb[0:1, 16:18]).then_inc(sem.l1, 16)
+    Y.dma_start(T.xch[q:q + 1, 0:2], T.cb[0:1, 2 * OWN:2 * OWN + 2]).then_inc(sem.l1, 16)
     nl1 = 16
 
-    hk = helpers_of(T, topo, k0)[q % 2]
-    for n in range(4):
-        k = order[n]
-        g.wait_ge(sem["qb%d" % n], 1)
-        if n in (1, 2):
-            nloc += send_pair(g, T, topo, core, q, k, T.qpc, T.qps, 256 * k)
-        else:
-            dst = hk if n == 0 else T.cores[partner]
-            ie = inner_engines(T, topo, core, dst)
-            rid, pid = topo.addr(dst)[0:2]
-            if n == 0:
-                a, w = 256 * k, 256
-                d, ds, s1, s2 = T.hc[:, 0:256], T.hs[:, 0:256], sem.hcs, sem.hss
-            else:
-                a, w = 128 * partner, 128
-                d, ds = T.lc[:, 128 * q:128 * q + 128], T.ls[:, 128 * q:128 * q + 128]
-                s1 = s2 = sem["pq%d" % q]
-            g.remote_dma(codes(d), codes(T.qpc[:, a:a + w]), s1, sem.loc, pid, rid, mask_of(ie))
-            g.remote_dma(ds, T.qps[:, a:a + w], s2, sem.loc, pid, rid, mask_of(ie))
-            nloc += 2 * len(ie)
-        if n == 1:
+    mine = slice(128 * q, 128 * q + 128)
+
+    def side(i, what):
+        r = seq[i]
+        a = slice(128 * r, 128 * r + 128)
+        s = T.qps[:, a] if what else codes(T.qpc[:, a])
+        if r in H:
+            n = H.index(r)
+            b = slice(128 * n, 128 * n + 128)
+            return hk, (T.hs[:, b] if what else codes(T.hc[:, b])), s, sem["hs%d" % n if what else "hc%d" % n]
+        return T.cores[r], (T.ls[:, mine] if what else codes(T.lc[:, mine])), s, sem["pq%d" % q]
+
+    def send(i, what, eng):
+        dst, d, s, rs = side(i, what)
+        return write(g, topo, dst, d, s, rs, sem.loc, eng)
+
+    for i in range(7):
+        eng = inp if i == 6 else (inh if seq[i] in H else out)
+        g.wait_ge(sem["qb%d" % i], 1)
+        nloc += send(i, 0, eng)
+        if i == 6:
+            nloc += send(i, 1, eng)
+        elif i % 2:
+            tr = []
+            for x, e in ((i - 1, inh), (i, out)):
+                dst, d, s, rs = side(x, 1)
+                tr.append(RemoteDMATransfer(dst_ids=[did(topo, dst)], dma_engine_mask=mask_of(e), remote_sem=rs, srcs=[s], dsts=[d]))
+                nloc += len(e)
+            g.remote_dma_fused(tr, local_sem=sem.loc)
+        if i == 2:
             g.wait_ge(sem.cho, 16)
-            g.remote_dma_fused([RemoteDMATransfer(dst_ids=ids, dma_engine_mask=mask_of(eng[:1]), remote_sem=sem.cha,
-                                                  srcs=[T.chd[q]], dsts=[T.chd[q] for r in others])], local_sem=sem.loc)
+            g.remote_dma_fused([RemoteDMATransfer(dst_ids=[did(topo, T.cores[r]) for r in others], dma_engine_mask=mask_of(out[:1]),
+                                                  remote_sem=sem.cha, srcs=[T.chd[q]], dsts=[T.chd[q] for r in others])],
+                               local_sem=sem.loc)
             nloc += 1
 
-    arrive = [order[1], order[3], order[2], order[0]]
+    Y.wait_ge(sem.cha, 7)
+    if q > 0:
+        a = 2 * (q - 1)
+        Y.dma_start(T.xch[0:q, 0:2], T.chd[0:q, a:a + 2, 0]).then_inc(sem.l1, 16)
+        nl1 += 16
+    if q < 7:
+        a = 2 * q
+        Y.dma_start(T.xch[q + 1:8, 0:2], T.chd[q + 1:8, a:a + 2, 0]).then_inc(sem.l1, 16)
+        nl1 += 16
+    Y.wait_ge(sem.l1, nl1)
+    for j in range(2):
+        Y.dma_start(T.ch[j:j + 1, :], T.xch[0:8, j:j + 1]).then_inc(sem.stc, 16)
+
+    arrive = [D[0], H[0], q, D[1], partner, H[1], D[2], H[2]]
     E.wait_ge(sem.qw, 1)
-    for n, k in enumerate(arrive):
-        if k == k0:
-            E.wait_ge(sem.qown, 1)
-            E.wait_ge(sem["pq%d" % partner], 2 * len(inner_engines(T, topo, T.cores[partner], core)))
+    E.wait_ge(sem.v0, 1)
+    for i, o in enumerate(arrive):
+        if o == q:
+            E.wait_ge(sem.qb7, 1)
+        elif o == partner:
+            E.wait_ge(sem["pq%d" % o], 2 * len(inner_engines(T, topo, T.cores[o], core)))
+        elif o in H:
+            E.wait_ge(sem["pq%d" % o], 2 * len(outer_engines(T, topo, helpers_of(T, topo, o // 2)[o % 2])))
         else:
-            for o in (2 * k, 2 * k + 1):
-                E.wait_ge(sem["pq%d" % o], len(topo.engines(T.cores[o], core)))
-        for j in range(2):
-            E.matmul_mx(T["ps%d" % (2 * k + j)][:, 0:256], T.qwc[:, 128 * j:128 * j + 128], T.qws[:, 128 * j:128 * j + 128],
-                        T.lc[:, 256 * k:256 * k + 256], T.ls[:, 256 * k:256 * k + 256], True, True).then_inc(
-                            sem["my%d%s" % (k, "ab"[j])], 1)
-        V.wait_ge(sem["my%da" % k], 1)
-        S.wait_ge(sem["my%db" % k], 1)
-        for h in range(2):
-            o = 2 * k + h
-            V.tensor_copy(T.ysb[:, 64 * o:64 * o + 64], T["ps%d" % (2 * k)][:, 128 * h:128 * h + 64]).then_inc(sem["ya%d" % k], 1)
-            S.activation(T.ysb[:, 64 * (8 + o):64 * (8 + o) + 64], T["ps%d" % (2 * k + 1)][:, 128 * h + 64:128 * h + 128],
-                         ActivationFunctionType.Copy).then_inc(sem["yb%d" % k], 1)
-        if n == 0:
-            Y.wait_ge(sem.cha, 7)
-            if q > 0:
-                a = 2 * (q - 1)
-                Y.dma_start(T.xch[0:q, 0:2], T.chd[0:q, a:a + 2, 0]).then_inc(sem.l1, 16)
-                nl1 += 16
-            if q < 7:
-                a = 2 * q
-                Y.dma_start(T.xch[q + 1:8, 0:2], T.chd[q + 1:8, a:a + 2, 0]).then_inc(sem.l1, 16)
-                nl1 += 16
-        c = 128 * k
-        Y.wait_ge(sem["ya%d" % k], 2)
+            E.wait_ge(sem["pq%d" % o], 2 * len(outer_engines(T, topo, T.cores[o])))
+        if i >= 4:
+            E.wait_ge(sem["ya%d" % (i - 4)], 1)
+            E.wait_ge(sem["yb%d" % (i - 4)], 1)
+        pa, pb = T["ps%d" % (2 * (i % 4))], T["ps%d" % (2 * (i % 4) + 1)]
+        for j, ps in enumerate((pa, pb)):
+            E.matmul_mx(ps[:, 0:128], T.qwc[:, 128 * j:128 * j + 128], T.qws[:, 128 * j:128 * j + 128],
+                        T.lc[:, 128 * o:128 * o + 128], T.ls[:, 128 * o:128 * o + 128], True, True).then_inc(
+                            sem["my%d%s" % (i, "ab"[j])], 1)
+        V.wait_ge(sem["my%da" % i], 1)
+        V.tensor_copy(T.ysb[:, 64 * o:64 * o + 64], pa[:, 0:64]).then_inc(sem["ya%d" % i], 1)
+        S.wait_ge(sem["my%db" % i], 1)
+        S.activation(T.ysb[:, 512 + 64 * o:512 + 64 * o + 64], pb[:, 64:128], ActivationFunctionType.Copy).then_inc(
+            sem["yb%d" % i], 1)
+        if (o ^ 1) not in arrive[:i]:
+            continue
+        c = 128 * (o // 2)
+        for x in (arrive.index(o ^ 1), i):
+            Y.wait_ge(sem["ya%d" % x], 1)
         Y.dma_start(T.y[:, c:c + 128], T.ysb[:, c:c + 128]).then_inc(sem.sty, 16)
-        S.wait_ge(sem["yb%d" % k], 2)
+        for x in (arrive.index(o ^ 1), i):
+            S.wait_ge(sem["yb%d" % x], 1)
         S.dma_start(T.y[:, 512 + c:512 + c + 128], T.ysb[:, 512 + c:512 + c + 128]).then_inc(sem.stz, 16)
-        if n == 1:
-            Y.wait_ge(sem.l1, nl1)
-            for j in range(2):
-                Y.dma_start(T.ch[j:j + 1, :], T.xch[0:8, j:j + 1]).then_inc(sem.stc, 16)
     Y.wait_ge(sem.sty, 64)
     Y.wait_ge(sem.stc, 32)
     S.wait_ge(sem.stz, 64)

from concourse.bass import DstId, RemoteDMATransfer
from concourse.mybir import dt, AluOpType, ActivationFunctionType

F8 = "float8_e4m3fn_x4"
SCRATCH = {
    "gt": ("sbuf", [128, 512], "bfloat16"),
    "gz": ("sbuf", [128, 512], "bfloat16"),
    "st": ("sbuf", [128, 512], "bfloat16"),
    "wt": ("sbuf", [128, 1024], "bfloat16"),
    "win": ("sbuf", [128, 4096], "bfloat16"),
    "pt": ("sbuf", [128, 4096], "bfloat16"),
    "sgc": ("sbuf", [128, 160], F8),
    "sgs": ("sbuf", [128, 160], "uint8"),
    "zc": ("sbuf", [128, 128], F8),
    "zs": ("sbuf", [128, 128], "uint8"),
    "smc": ("sbuf", [128, 128], F8),
    "sms": ("sbuf", [128, 128], "uint8"),
    "qwc": ("sbuf", [128, 256], F8),
    "qws": ("sbuf", [128, 256], "uint8"),
    "qpc": ("sbuf", [128, 1024], F8),
    "qps": ("sbuf", [128, 1024], "uint8"),
    "lc": ("sbuf", [128, 1024], F8),
    "ls": ("sbuf", [128, 1024], "uint8"),
    "hc": ("sbuf", [128, 384], F8),
    "hs": ("sbuf", [128, 384], "uint8"),
    "ia": ("sbuf", [128, 16], "int32"),
    "ib": ("sbuf", [128, 16], "int32"),
    "ic": ("sbuf", [128, 16], "int32"),
    "bs": ("sbuf", [128, 16], "float32"),
    "base": ("sbuf", [128, 16], "float32"),
    "neg": ("sbuf", [128, 16], "float32"),
    "z32": ("sbuf", [128, 32], "float32"),
    "sct": ("sbuf", [128, 32], "float32"),
    "run": ("sbuf", [128, 16], "float32"),
    "lt": ("sbuf", [128, 16], "float32"),
    "cc": ("sbuf", [128, 1], "float32"),
    "rep": ("sbuf", [128, 32], "float32"),
    "cb": ("sbuf", [128, 128], "float32"),
    "off": ("sbuf", [128, 256], "uint16"),
    "xch": ("sbuf", [128, 2], "float32"),
    "ysb": ("sbuf", [128, 1024], "float32"),
    "chd": ("dram", [8, 128, 1], "float32"),
}
for _b in range(8):
    SCRATCH["ps%d" % _b] = ("psum", [128, 512], "float32")

SEMAPHORES = ["mz", "ms", "qz", "lgs", "qg", "lsm", "cps", "qs", "i1", "i2", "b1", "b2", "b3", "lpg", "lqw", "qw", "gsa", "go",
              "sc", "v0", "v1", "v3", "v4", "v5", "cho", "cha", "l1", "stc", "sty", "stz", "loc"]
for _i in range(8):
    SEMAPHORES += ["oa%d" % _i, "gv%d" % _i, "gx%d" % _i, "qb%d" % _i, "my%da" % _i, "my%db" % _i, "ya%d" % _i, "yb%d" % _i,
                   "pq%d" % _i]
for _n in range(3):
    SEMAPHORES += ["hc%d" % _n, "hs%d" % _n]

NP = 4
CUT = 10
FIRST = 14
OWN = 9


def mask_of(eng):
    m = 0
    for e in eng:
        m |= 1 << e
    return m


def did(topo, c):
    a = topo.addr(c)
    return DstId(rid=a[0], pnc=a[1])


def rounds_of(T, topo):
    ch = [topo.chip(T.cores[2 * k]) for k in range(NP)]
    return sorted([1, 2, 3], key=lambda s: (topo.same_plane(ch[0], ch[s]), s))


def far_of(T, topo, c):
    return [f for f in T.cores if topo.chip(f) != topo.chip(c)]


def helpers_of(T, topo, k):
    a = T.cores[2 * k]
    return [c for c in topo.cores_of(a) if topo.die(c) != topo.die(a) and all(topo.may_write(c, f) for f in far_of(T, topo, a))]


def outer_engines(T, topo, src):
    far = far_of(T, topo, src)
    return [e for e in topo.engines(src, far[0]) if all(e in topo.engines(src, f) for f in far)]


def inner_engines(T, topo, src, dst):
    out = outer_engines(T, topo, src)
    return [e for e in topo.engines(src, dst) if e not in out]


def codes(ap):
    return ap.bitcast(dt.uint8)


def write(g, topo, dst, d, s, rsem, lsem, eng):
    rid, pid = topo.addr(dst)[0:2]
    g.remote_dma(d, s, rsem, lsem, pid, rid, mask_of(eng))
    return len(eng)


def zeros_to(g, T, topo, dst, col, eng):
    sem = T.sem
    g.vector.memset(T.gz[:], 0.0).then_inc(sem.mz, 1)
    g.vector.wait_ge(sem.mz, 1)
    g.vector.quantize_mx(T.zc[:], T.zs[:], T.gz[:]).then_inc(sem.qz, 1)
    g.wait_ge(sem.qz, 1)
    n = write(g, topo, dst, codes(T.sgc[:, col:col + 2]), codes(T.zc[:, 0:2]), sem.gsa, sem.loc, eng)
    n += write(g, topo, dst, T.sgs[:, col:col + 2], T.zs[:, 0:2], sem.gsa, sem.loc, eng)
    return n


def helper_program(g, core, T, topo, q, rounds):
    sem = T.sem
    out = outer_engines(T, topo, core)
    n8 = len(inner_engines(T, topo, T.cores[q], core))
    nloc = zeros_to(g, T, topo, T.cores[q], FIRST + 16, out)
    for n in range(3):
        r = 2 * ((q // 2) ^ rounds[n]) + 1 - q % 2
        a, b = 128 * n, 128 * q
        g.wait_ge(sem["hc%d" % n], n8)
        nloc += write(g, topo, T.cores[r], codes(T.lc[:, b:b + 128]), codes(T.hc[:, a:a + 128]), sem["pq%d" % q], sem.loc, out)
        g.wait_ge(sem["hs%d" % n], n8)
        nloc += write(g, topo, T.cores[r], T.ls[:, b:b + 128], T.hs[:, a:a + 128], sem["pq%d" % q], sem.loc, out)
    g.wait_ge(sem.loc, nloc)


def rank_program(g, core, T, topo):
    sem = T.sem
    rounds = rounds_of(T, topo)
    rank = T.rank_of(core)
    if rank is None:
        for k in range(NP):
            hs = helpers_of(T, topo, k)
            for h in range(2):
                if core == hs[h]:
                    helper_program(g, core, T, topo, 2 * k + h, rounds)
        return
    q = rank
    k0, par = q // 2, q % 2
    partner = q ^ 1
    hk = helpers_of(T, topo, k0)[par]
    slot = lambda r, o: OWN if r == o else (r if r < o else r - 1)
    others = [r for r in range(8) if r != q]
    far = [r for r in others if r != partner]
    out = outer_engines(T, topo, core)
    inp = inner_engines(T, topo, core, T.cores[partner])
    inh = inner_engines(T, topo, core, hk)
    V, S, Y, E = g.vector, g.scalar, g.sync, g.tensor
    H = [2 * (k0 ^ s) + 1 - par for s in rounds]
    D = [2 * (k0 ^ s) + par for s in rounds]
    seq = [H[0], D[0], H[1], D[1], H[2], D[2], partner, q]

    def page(eng, m):
        eng.dma_start(T.win[:, 256 * m:256 * m + 256], T.pg[128 * m:128 * m + 128, :]).then_inc(sem.lpg, 16)

    Y.dma_start(T.gt[:, 0:8], T.gs[:, 0:8]).then_inc(sem.lgs, 16)
    S.dma_start(T.st[:, 0:64], T.sm[:, 0:64]).then_inc(sem.lsm, 16)
    for m in range(4):
        page(Y, m)
        page(S, 4 + m)
    Y.wait_ge(sem.go, 1)
    S.wait_ge(sem.go, 1)
    for m in range(8, 12):
        page(Y, m)
        page(S, 4 + m)
    Y.dma_start(T.wt[:], T.qw[:]).then_inc(sem.lqw, 16)

    nloc = zeros_to(g, T, topo, T.cores[partner], FIRST + 14, topo.engines(core, T.cores[partner]))
    V.memset(T.gt[:, 8:512], 0.0).then_inc(sem.ms, 1)
    V.memset(T.st[:, 64:512], 0.0).then_inc(sem.ms, 1)
    V.memset(T.neg[:], -9.0e29).then_inc(sem.ms, 1)
    V.memset(T.z32[:], 0.0).then_inc(sem.ms, 1)
    V.memset(T.cb[:, 32:128], 0.0).then_inc(sem.ms, 1)
    V.wait_ge(sem.ms, 5)
    V.wait_ge(sem.lgs, 16)
    V.quantize_mx(T.sgc[:, 32:160], T.sgs[:, 32:160], T.gt[:]).then_inc(sem.qg, 1)
    V.wait_ge(sem.lsm, 16)
    for b in range(1, 4):
        V.tensor_copy(T.st[:, 128 * b:128 * b + 64], T.st[:, 0:64]).then_inc(sem.cps, 1)
    V.wait_ge(sem.cps, 3)
    V.quantize_mx(T.smc[:], T.sms[:], T.st[:]).then_inc(sem.qs, 1)

    g.wait_ge(sem.qg, 1)
    for what in range(2):
        tr = []
        for dst, eng in ((far, out), ([partner], inp)):
            at = [FIRST + 2 * slot(q, r) for r in dst]
            if what == 0:
                s, d = codes(T.sgc[:, 32:34]), [codes(T.sgc[:, a:a + 2]) for a in at]
            else:
                s, d = T.sgs[:, 32:34], [T.sgs[:, a:a + 2] for a in at]
            tr.append(RemoteDMATransfer(dst_ids=[did(topo, T.cores[r]) for r in dst], dma_engine_mask=mask_of(eng),
                                        remote_sem=sem.gsa, srcs=[s], dsts=d))
            nloc += len(eng)
        g.remote_dma_fused(tr, local_sem=sem.loc)
    g.sem_inc(sem.go, 1)

    g.iota(T.ia[:], [[0, 16]], 0, 1).then_inc(sem.i1, 1)
    g.iota(T.ib[:], [[16, 16]], 0, 0).then_inc(sem.i2, 1)
    V.wait_ge(sem.i1, 1)
    V.tensor_scalar(T.ic[:], T.ia[:], 15, None, AluOpType.bitwise_and).then_inc(sem.b1, 1)
    V.wait_ge(sem.i2, 1)
    V.wait_ge(sem.b1, 1)
    V.tensor_tensor(T.bs[:], T.ic[:], T.ib[:], AluOpType.add).then_inc(sem.b2, 1)
    V.wait_ge(sem.b2, 1)
    V.tensor_scalar(T.base[:], T.bs[:], 1.0 / 256.0, None, AluOpType.mult).then_inc(sem.b3, 1)
    V.wait_ge(sem.b3, 1)

    narr = 0
    for r in far:
        narr += 2 * len(outer_engines(T, topo, T.cores[r]))
    narr += 2 * len(inner_engines(T, topo, T.cores[partner], core)) + 2 * len(topo.engines(T.cores[partner], core))
    narr += 2 * len(outer_engines(T, topo, hk))
    E.wait_ge(sem.qg, 1)
    E.wait_ge(sem.qs, 1)
    E.wait_ge(sem.gsa, narr)
    score = T.ps6
    E.matmul_mx(score[:, 0:128], T.smc[:], T.sms[:], T.sgc[:, FIRST:FIRST + 128], T.sgs[:, FIRST:FIRST + 128], True, True).then_inc(
        sem.sc, 1)

    V.wait_ge(sem.sc, 1)
    V.transpose(T.sct[:], score[:, 0:32]).then_inc(sem.v0, 1)
    V.wait_ge(sem.v0, 1)
    V.tensor_tensor_scan(T.run[:], T.sct[:, 0:16], T.neg[:], -9.0e29, AluOpType.max, AluOpType.max).then_inc(sem.v1, 1)
    S.wait_ge(sem.v1, 1)
    S.activation(T.lt[:], T.run[:], ActivationFunctionType.Sign, bias=T.run[:, 15:16], scale=-1.0,
                 accum_out=T.cc[:, 0:1]).then_inc(sem.v3, 1)
    V.wait_ge(sem.v3, 1)
    V.tensor_scalar(T.rep[:], T.z32[:], T.cc[:, 0:1], None, AluOpType.add).then_inc(sem.v4, 1)
    V.wait_ge(sem.v4, 1)
    V.transpose(T.cb[:, 0:32], T.rep[:]).then_inc(sem.v5, 1)
    V.wait_ge(sem.v5, 1)

    def lists(i):
        r = seq[i]
        for j in range(2):
            c, o = 2 * slot(r, q) + j, 32 * r + 16 * j
            V.tensor_scalar(T.off[:, o:o + 16], T.base[:], T.cb[:, c:c + 1], 256.0, AluOpType.add,
                            AluOpType.mult).then_inc(sem["oa%d" % i], 1)

    lists(0)
    for i, r in enumerate(seq):
        o = 32 * r
        if i == 0:
            V.wait_ge(sem.lpg, 256)
            S.wait_ge(sem.lpg, 256)
        V.wait_ge(sem["oa%d" % i], 2)
        V.tensor_copy(T.pt[:, 16 * o:16 * (o + CUT)], T.win[:, 0:4096].indirect(T.off[:, o:o + CUT])).then_inc(sem["gv%d" % i], 1)
        S.wait_ge(sem["oa%d" % i], 2)
        S.activation(T.pt[:, 16 * (o + CUT):16 * (o + 32)], T.win[:, 0:4096].indirect(T.off[:, o + CUT:o + 32]),
                     ActivationFunctionType.Copy).then_inc(sem["gx%d" % i], 1)
        if i < 7:
            lists(i + 1)
        V.wait_ge(sem["gv%d" % i], 1)
        V.wait_ge(sem["gx%d" % i], 1)
        c, s = (T.lc, T.ls) if r == q else (T.qpc, T.qps)
        V.quantize_mx(c[:, 128 * r:128 * r + 128], s[:, 128 * r:128 * r + 128],
                      T.pt[:, 512 * r:512 * r + 512]).then_inc(sem["qb%d" % i], 1)
        if i == 5:
            V.wait_ge(sem.lqw, 16)
            V.quantize_mx(T.qwc[:], T.qws[:], T.wt[:]).then_inc(sem.qw, 1)

    Y.wait_ge(sem.v5, 1)
    Y.wait_ge(sem.ms, 5)
    Y.dma_start(T.chd[q], T.cb[0:1, 0:128]).then_inc(sem.cho, 16)
    Y.dma_start(T.xch[q:q + 1, 0:2], T.cb[0:1, 2 * OWN:2 * OWN + 2]).then_inc(sem.l1, 16)
    nl1 = 16

    mine = slice(128 * q, 128 * q + 128)

    def side(i, what):
        r = seq[i]
        a = slice(128 * r, 128 * r + 128)
        s = T.qps[:, a] if what else codes(T.qpc[:, a])
        if r in H:
            n = H.index(r)
            b = slice(128 * n, 128 * n + 128)
            return hk, (T.hs[:, b] if what else codes(T.hc[:, b])), s, sem["hs%d" % n if what else "hc%d" % n]
        return T.cores[r], (T.ls[:, mine] if what else codes(T.lc[:, mine])), s, sem["pq%d" % q]

    def send(i, what, eng):
        dst, d, s, rs = side(i, what)
        return write(g, topo, dst, d, s, rs, sem.loc, eng)

    for i in range(7):
        eng = inp if i == 6 else (inh if seq[i] in H else out)
        g.wait_ge(sem["qb%d" % i], 1)
        nloc += send(i, 0, eng)
        if i == 6:
            nloc += send(i, 1, eng)
        elif i % 2:
            tr = []
            for x, e in ((i - 1, inh), (i, out)):
                dst, d, s, rs = side(x, 1)
                tr.append(RemoteDMATransfer(dst_ids=[did(topo, dst)], dma_engine_mask=mask_of(e), remote_sem=rs, srcs=[s], dsts=[d]))
                nloc += len(e)
            g.remote_dma_fused(tr, local_sem=sem.loc)
        if i == 2:
            g.wait_ge(sem.cho, 16)
            g.remote_dma_fused([RemoteDMATransfer(dst_ids=[did(topo, T.cores[r]) for r in others], dma_engine_mask=mask_of(out[:1]),
                                                  remote_sem=sem.cha, srcs=[T.chd[q]], dsts=[T.chd[q] for r in others])],
                               local_sem=sem.loc)
            nloc += 1

    Y.wait_ge(sem.cha, 7)
    if q > 0:
        a = 2 * (q - 1)
        Y.dma_start(T.xch[0:q, 0:2], T.chd[0:q, a:a + 2, 0]).then_inc(sem.l1, 16)
        nl1 += 16
    if q < 7:
        a = 2 * q
        Y.dma_start(T.xch[q + 1:8, 0:2], T.chd[q + 1:8, a:a + 2, 0]).then_inc(sem.l1, 16)
        nl1 += 16
    Y.wait_ge(sem.l1, nl1)
    for j in range(2):
        Y.dma_start(T.ch[j:j + 1, :], T.xch[0:8, j:j + 1]).then_inc(sem.stc, 16)

    arrive = [D[0], H[0], q, D[1], partner, H[1], D[2], H[2]]
    E.wait_ge(sem.qw, 1)
    E.wait_ge(sem.v0, 1)
    for i, o in enumerate(arrive):
        if o == q:
            E.wait_ge(sem.qb7, 1)
        elif o == partner:
            E.wait_ge(sem["pq%d" % o], 2 * len(inner_engines(T, topo, T.cores[o], core)))
        elif o in H:
            E.wait_ge(sem["pq%d" % o], 2 * len(outer_engines(T, topo, helpers_of(T, topo, o // 2)[o % 2])))
        else:
            E.wait_ge(sem["pq%d" % o], 2 * len(outer_engines(T, topo, T.cores[o])))
        if i >= 4:
            E.wait_ge(sem["ya%d" % (i - 4)], 1)
            E.wait_ge(sem["yb%d" % (i - 4)], 1)
        pa, pb = T["ps%d" % (2 * (i % 4))], T["ps%d" % (2 * (i % 4) + 1)]
        for j, ps in enumerate((pa, pb)):
            E.matmul_mx(ps[:, 0:128], T.qwc[:, 128 * j:128 * j + 128], T.qws[:, 128 * j:128 * j + 128],
                        T.lc[:, 128 * o:128 * o + 128], T.ls[:, 128 * o:128 * o + 128], True, True).then_inc(
                            sem["my%d%s" % (i, "ab"[j])], 1)
        V.wait_ge(sem["my%da" % i], 1)
        V.tensor_copy(T.ysb[:, 64 * o:64 * o + 64], pa[:, 0:64]).then_inc(sem["ya%d" % i], 1)
        S.wait_ge(sem["my%db" % i], 1)
        S.activation(T.ysb[:, 512 + 64 * o:512 + 64 * o + 64], pb[:, 64:128], ActivationFunctionType.Copy).then_inc(
            sem["yb%d" % i], 1)
        if (o ^ 1) not in arrive[:i]:
            continue
        c = 128 * (o // 2)
        for x in (arrive.index(o ^ 1), i):
            Y.wait_ge(sem["ya%d" % x], 1)
        Y.dma_start(T.y[:, c:c + 128], T.ysb[:, c:c + 128]).then_inc(sem.sty, 16)
        for x in (arrive.index(o ^ 1), i):
            S.wait_ge(sem["yb%d" % x], 1)
        S.dma_start(T.y[:, 512 + c:512 + c + 128], T.ysb[:, 512 + c:512 + c + 128]).then_inc(sem.stz, 16)
    Y.wait_ge(sem.sty, 64)
    Y.wait_ge(sem.stc, 32)
    S.wait_ge(sem.stz, 64)
    g.wait_ge(sem.loc, nloc)
